import numpy as np
import ml_dtypes


def mxq(x, axis, fmt="e4m3"):
    dtype, down = {"e4m3": (ml_dtypes.float8_e4m3fn, 7), "e5m2": (ml_dtypes.float8_e5m2, 14)}[fmt]
    v = np.moveaxis(np.asarray(x, np.float32).astype(ml_dtypes.bfloat16).astype(np.float64), axis, -1)
    blocks = v.reshape(v.shape[:-1] + (-1, 32))
    amax = np.abs(blocks).max(-1, keepdims=True)
    byte = np.maximum(np.where(amax > 0, np.frexp(amax)[1] - 1 + 127, 0) - down, 1)
    scale = np.exp2(byte - 127.0)
    codes = (blocks / scale).astype(np.float32).astype(dtype).astype(np.float64)
    return np.moveaxis((codes * scale).reshape(v.shape), -1, axis)


WIDE = False


def mx_kscale(k):
    if not WIDE:
        return np.ones(k)
    levels = np.array([10, -10, 5, -5, 0])
    if k % 512:
        return np.exp2(np.random.permutation(np.resize(levels, k // 32))).repeat(32)
    a = np.empty((k // 512, 16))
    for p in range(k // 512):
        a[p, :8] = np.random.permutation(np.resize(levels, 8))
        for g in range(8):
            far = levels[np.abs(levels - a[p, g]) >= 10]
            a[p, g + 8] = far[np.random.randint(len(far))]
    return np.exp2(a.ravel()).repeat(32)


def f64(x):
    return np.asarray(x).astype(np.float64)


def striped(idx):
    return np.tile(idx.reshape(-1, 16).T, (8, 1)).astype(np.uint16)


def unstriped(offs):
    return offs[:16].T.reshape(-1).astype(np.int64)


E2M1 = np.array([0.0, 0.5, 1.0, 1.5, 2.0, 3.0, 4.0, 6.0, -0.0, -0.5, -1.0, -1.5, -2.0, -3.0, -4.0, -6.0])


def pack_weight(w, fmt):
    k, n = w.shape
    w = f64(np.asarray(w, np.float32).astype(ml_dtypes.bfloat16)).reshape(k // 32, 32, n)
    amax = np.abs(w).max(1)
    if fmt == "e4m3":
        byte = np.frexp(amax)[1] - 1 + 127 - 7
    else:
        mant, ex = np.frexp(amax / 6.0)
        byte = np.where(mant > 0.5, ex, ex - 1) + 127
    byte = np.clip(np.where(amax > 0, byte, 1), 1, 254)
    scaled = (w * np.exp2(127.0 - byte)[:, None, :]).reshape(k, n).astype(np.float32)
    by_word = np.ascontiguousarray(scaled.reshape(k // 512, 128, 4, n).transpose(0, 1, 3, 2))
    if fmt == "e4m3":
        words = by_word.astype(ml_dtypes.float8_e4m3fn).view(np.uint8)
    else:
        c = by_word.astype(ml_dtypes.float4_e2m1fn).view(np.uint8) & 0xF
        words = (c[..., 0::2] | (c[..., 1::2] << 4)).reshape(k // 512, 128, 2 * n)
    return np.ascontiguousarray(words), np.ascontiguousarray(byte.astype(np.uint8).reshape(k // 512, 16, n))


def unpack_weight(words, scales, fmt):
    g, _, n = scales.shape
    words = np.ascontiguousarray(words).reshape(g, 128, n, -1)
    if fmt == "e4m3":
        vals = words.view(ml_dtypes.float8_e4m3fn).astype(np.float64)
    else:
        nib = np.empty((g, 128, n, 4), np.uint8)
        nib[..., 0::2] = words & 0xF
        nib[..., 1::2] = words >> 4
        vals = E2M1[nib]
    vals = vals * np.repeat(np.exp2(scales.astype(np.float64) - 127.0), 8, axis=1)[..., None]
    return vals.transpose(0, 1, 3, 2).reshape(g * 512, n)


def gelu(v):
    return 0.5 * v * (1.0 + np.tanh(np.sqrt(2.0 / np.pi) * (v + 0.044715 * v**3)))


K, K2, H, N, T, S = 1024, 512, 1024, 512, 2048, 1024


def setup_inputs():
    n = np.random.standard_normal
    s = mx_kscale(K)[:, None]
    s2 = mx_kscale(K2)[:, None]
    u = mx_kscale(H)[:, None]
    d = {}
    d["tab_words"], d["tab_scales"] = pack_weight(n((K, T)) * s, "e4m3")
    d["offs"] = striped(np.random.permutation(T)[:S])
    d["xs_words"], d["xs_scales"] = pack_weight(n((K2, S)) * s2, "e4m3")
    d["wa"] = (n((K, H)) / s / K ** 0.5).astype(np.float32)
    d["wb_words"], d["wb_scales"] = pack_weight(n((K2, H)) / s2 / K2 ** 0.5, "e2m1")
    d["gain"] = (np.exp(0.3 * n(H)) * u[:, 0]).astype(np.float32)
    d["wo"] = (2.0 * n((H, N)) / u / H ** 0.5).astype(np.float32)
    d["wd_words"], d["wd_scales"] = pack_weight(0.7 * n((K, N)) / s / K ** 0.5, "e4m3")
    d["bo"] = (0.5 * n(N)).astype(np.float32)
    return d


def reference(tab_words, tab_scales, offs, xs_words, xs_scales, wa, wb_words, wb_scales,
              gain, wo, wd_words, wd_scales, bo):
    v = unpack_weight(tab_words, tab_scales, "e4m3")[:, unstriped(offs)]
    xs = unpack_weight(xs_words, xs_scales, "e4m3")
    wb = unpack_weight(wb_words, wb_scales, "e2m1")
    wd = unpack_weight(wd_words, wd_scales, "e4m3")
    a = mxq(f64(wa), 0, "e4m3").T @ v
    b = wb.T @ xs
    near = np.exp(-np.abs(a - b))
    h = a * near * f64(gain)[:, None]
    y = mxq(f64(wo), 0, "e4m3").T @ mxq(h, 0, "e4m3") + wd.T @ v
    return y + f64(bo)[:, None]

@@ -1,0 +1,297 @@
+from contextlib import ExitStack
+
+import concourse.mybir as mybir
+
+K, K2, H, N, T, S = 1024, 512, 1024, 512, 2048, 1024
+FLOPS = 2 * S * (K * H + K2 * H + H * N + K * N)
+
+F32 = mybir.dt.float32
+BF16 = mybir.dt.bfloat16
+I32 = mybir.dt.int32
+U32 = mybir.dt.uint32
+U16 = mybir.dt.uint16
+U8 = mybir.dt.uint8
+FP8X4 = mybir.dt.float8_e4m3fn_x4
+FP4X4 = mybir.dt.float4_e2m1fn_x4
+ALU = mybir.AluOpType
+ACT = mybir.ActivationFunctionType
+
+P = 128
+PACK = 4
+PASS = P * PACK
+BANK = 512
+UNITS = [(0, 0, 512), (0, 512, 512), (1, 0, 512), (1, 512, 256), (1, 768, 256)]
+
+
+def tile_list_anaesthesia_depth_agreement_kernel(
+    tc, tab_words, tab_scales, offs, xs_words, xs_scales, wa, wb_words, wb_scales,
+    gain, wo, wd_words, wd_scales, bo, out,
+):
+    nc = tc.nc
+    with ExitStack() as ctx:
+        keep = ctx.enter_context(tc.tile_pool(name="keep", bufs=1))
+        ring = ctx.enter_context(tc.tile_pool(name="ring", bufs=4))
+        psum = ctx.enter_context(tc.psum_pool(name="psum", bufs=4))
+
+        def held(shape, dtype, name):
+            return keep.tile(shape, dtype, name=name, align_bytes=64)
+
+        offsets = held([P, S // 16], U16, "offsets")
+        tab_w = [held([P, T], I32, "tab_w%d" % a) for a in range(2)]
+        tab_s = held([P, T], U8, "tab_s")
+        wb_raw_w = held([P, 2 * H], U8, "wb_raw_w")
+        wb_rows_s = held([P, H], U8, "wb_rows_s")
+        wb_raw_s = held([P, H], U8, "wb_raw_s")
+        wb_w = held([P, 2 * H], U8, "wb_w")
+        wb_s = held([P, H], U8, "wb_s")
+        xs_w = held([P, S], I32, "xs_w")
+        xs_s = held([P, S], U8, "xs_s")
+        wd_w = held([P, 2, N], I32, "wd_w")
+        wd_s = held([P, N], U8, "wd_s")
+        gains = held([P, 2, PACK], F32, "gains")
+        biases = held([P, N // P], F32, "biases")
+        wa_raw = {(a, b): held([P, PACK, PASS], F32, "wa_raw%d%d" % (a, b)) for b in range(2) for a in range(2)}
+        wo_raw = [held([P, PACK, N], F32, "wo_raw%d" % b) for b in range(2)]
+
+        nc.vector.memset(wb_raw_s[:].bitcast(I32), 0)
+        nc.gpsimd.memset(tab_s[:].bitcast(I32), 0)
+
+        def load_scale_quadrant(queue, plane, scales, q):
+            passes = scales.shape[0]
+            queue.dma_start(
+                out=plane[32 * q : 32 * q + 4 * passes, :].bitcast(I32),
+                in_=scales[:, 4 * q : 4 * q + 4, :].bitcast(I32),
+            )
+
+        def load_scale_rows(queue, plane, scales):
+            for q in range(4):
+                load_scale_quadrant(queue, plane, scales, q)
+
+        def load_words(tile, words):
+            nc.sync.dma_start(out=tile, in_=words.rearrange("p c i -> p (c i)").bitcast(I32))
+
+        def load_wa(a, b):
+            rows = wa[a * PASS : (a + 1) * PASS, b * PASS : (b + 1) * PASS]
+            nc.sync.dma_start(out=wa_raw[a, b][:], in_=rows.rearrange("(p j) c -> p j c", j=PACK))
+
+        nc.sync.dma_start(out=wb_raw_w[:].bitcast(I32), in_=wb_words[0].bitcast(I32))
+        load_scale_quadrant(nc.scalar, wb_rows_s, wb_scales, 0)
+        load_words(xs_w[:], xs_words[0])
+        load_scale_quadrant(nc.scalar, wb_rows_s, wb_scales, 1)
+        load_words(tab_w[0][:], tab_words[0])
+        load_scale_quadrant(nc.scalar, wb_rows_s, wb_scales, 2)
+        nc.sync.dma_start(offsets[:], offs)
+        load_scale_quadrant(nc.scalar, wb_rows_s, wb_scales, 3)
+        load_words(tab_w[1][:], tab_words[1])
+        load_scale_quadrant(nc.scalar, xs_s, xs_scales, 0)
+        load_wa(0, 0)
+        load_scale_quadrant(nc.scalar, xs_s, xs_scales, 1)
+        load_wa(1, 0)
+        load_scale_quadrant(nc.scalar, xs_s, xs_scales, 2)
+        nc.sync.dma_start(out=gains[:], in_=gain.rearrange("(b p t) -> p b t", p=P, t=PACK))
+        load_scale_quadrant(nc.scalar, xs_s, xs_scales, 3)
+        load_wa(0, 1)
+        load_wa(1, 1)
+        nc.sync.dma_start(out=wd_w[:], in_=wd_words.rearrange("a p c i -> p a (c i)").bitcast(I32))
+        load_scale_rows(nc.sync, wd_s, wd_scales)
+        for b in range(2):
+            rows = wo[b * PASS : (b + 1) * PASS, :]
+            nc.sync.dma_start(out=wo_raw[b][:], in_=rows.rearrange("(p j) c -> p j c", j=PACK))
+        with nc.allow_non_contiguous_dma(reason="one bias value a partition"):
+            nc.sync.dma_start(out=biases[:], in_=bo.rearrange("(t p) -> p t", p=P))
+        load_scale_rows(nc.gpsimd, tab_s, tab_scales)
+
+        for q in range(4):
+            rows = slice(32 * q, 32 * q + 4)
+            nc.vector.tensor_copy(out=wb_raw_s[rows, :].bitcast(I32), in_=wb_rows_s[rows, :].bitcast(I32))
+        nc.vector.tensor_copy(
+            out=wb_w[:].bitcast(U16).rearrange("p (b t m) -> p b t m", b=2, t=PACK),
+            in_=wb_raw_w[:].bitcast(U16).rearrange("p (b m t) -> p b t m", b=2, t=PACK),
+        )
+        nc.vector.tensor_copy(
+            out=wb_s[:].rearrange("p (b t m) -> p b t m", b=2, t=PACK),
+            in_=wb_raw_s[:].rearrange("p (b m t) -> p b t m", b=2, t=PACK),
+        )
+
+        steps = []
+        for u, (b, c0, width) in enumerate(UNITS):
+            per_bank = BANK // width
+            for t0 in range(0, PACK, per_bank):
+                steps.append((u, b, c0, width, list(range(t0, t0 + per_bank))))
+
+        b_sb = []
+        for s, (u, b, c0, width, slots) in enumerate(steps):
+            bank = psum.tile([P, BANK], F32, name="bank_by", tag="bank_by")
+            for g, t in enumerate(slots):
+                col = b * PASS + t * P
+                nc.tensor.matmul_mx(
+                    out=bank[:, g * width : (g + 1) * width],
+                    lhsT=wb_w[:, 2 * col : 2 * (col + P)].bitcast(FP4X4),
+                    lhsT_scale=wb_s[:, col : col + P],
+                    rhs=xs_w[:, c0 : c0 + width].bitcast(FP8X4),
+                    rhs_scale=xs_s[:, c0 : c0 + width],
+                    start=True,
+                    stop=True,
+                )
+            kept = held([P, BANK], F32, "b_sb%d" % s)
+            nc.scalar.activation(out=kept[:], in_=bank[:], func=ACT.Copy)
+            b_sb.append(kept)
+
+        v_w = {}
+        v_s = {}
+
+        def gather_words(a, half):
+            v_w[a, half] = held([P, BANK], U32, "v_w%d%d" % (a, half))
+            part = offsets[:, 32 * half : 32 * (half + 1)]
+            nc.vector.tensor_copy(v_w[a, half][:], tab_w[a][:].bitcast(U32).indirect(part))
+
+        def gather_scales(half):
+            v_s[half] = held([P, BANK], U8, "v_s%d" % half)
+            part = offsets[:, 32 * half : 32 * (half + 1)]
+            nc.vector.tensor_copy(v_s[half][:], tab_s[:].indirect(part))
+
+        def cast(engine, dst, src):
+            if engine is nc.gpsimd:
+                nc.gpsimd.tensor_scalar(dst, src, 1.0, 0.0, ALU.mult, ALU.add)
+            else:
+                nc.vector.tensor_copy(out=dst, in_=src)
+
+        wa_q = {}
+
+        def round_wa(a, b, part, engine):
+            grouped = held([P, 2, P, PACK], BF16, "wa_bf%d%d%d" % (a, b, part))
+            src = wa_raw[a, b][:].rearrange("p j (m t) -> p t m j", t=PACK)[:, 2 * part : 2 * part + 2]
+            cast(engine, grouped[:], src)
+            return grouped
+
+        def quantise(name, grouped_flat, words):
+            codes = held([P, words], U32, name + "_w")
+            scales = held([P, words], U8, name + "_s")
+            nc.vector.quantize_mx(out=codes[:].bitcast(FP8X4), scales=scales[:], in_=grouped_flat)
+            return codes, scales
+
+        def quantise_wa(a, b, part, grouped):
+            wa_q[a, b, part] = quantise("wa%d%d%d" % (a, b, part), grouped[:].rearrange("p t m j -> p (t m j)"), 2 * P)
+
+        for a in range(2):
+            for half in range(2):
+                gather_words(a, half)
+        for half in range(2):
+            gather_scales(half)
+        first = [round_wa(0, 0, part, nc.gpsimd) for part in range(2)]
+        second = [round_wa(1, 0, 0, nc.vector), round_wa(1, 0, 1, nc.gpsimd)]
+        for part in range(2):
+            quantise_wa(0, 0, part, first[part])
+            quantise_wa(1, 0, part, second[part])
+
+        wo_q = {}
+
+        def prepare_wa_block1():
+            for a in range(2):
+                for part in range(2):
+                    quantise_wa(a, 1, part, round_wa(a, 1, part, nc.gpsimd))
+
+        def prepare_wo(b):
+            grouped = held([P, N, PACK], BF16, "wo_bf%d" % b)
+            cast(nc.gpsimd, grouped[:], wo_raw[b][:].rearrange("p j c -> p c j"))
+            wo_q[b] = quantise("wo%d" % b, grouped[:].rearrange("p c j -> p (c j)"), N)
+
+        h_rows = {}
+        h_q = {}
+        a_banks = {}
+        nears = {}
+
+        def window(c0, width):
+            half, lo = divmod(c0, BANK)
+            return half, slice(lo, lo + width)
+
+        def front(s):
+            u, b, c0, width, slots = steps[s]
+            half, cols = window(c0, width)
+            bank = psum.tile([P, BANK], F32, name="bank_a", tag="bank_a")
+            for g, t in enumerate(slots):
+                part, m0 = t // 2, (t % 2) * P
+                for a in range(2):
+                    codes, scales = wa_q[a, b, part]
+                    nc.tensor.matmul_mx(
+                        out=bank[:, g * width : (g + 1) * width],
+                        lhsT=codes[:, m0 : m0 + P].bitcast(FP8X4),
+                        lhsT_scale=scales[:, m0 : m0 + P],
+                        rhs=v_w[a, half][:, cols].bitcast(FP8X4),
+                        rhs_scale=v_s[half][4 * a :, cols],
+                        start=(a == 0),
+                        stop=(a == 1),
+                    )
+            diff = ring.tile([P, BANK], F32, name="diff")
+            nc.vector.tensor_tensor(diff[:], bank[:], b_sb[s][:], ALU.subtract)
+            dist = ring.tile([P, BANK], F32, name="dist")
+            nc.scalar.activation(out=dist[:], in_=diff[:], func=ACT.Abs)
+            near = ring.tile([P, BANK], F32, name="near")
+            nc.scalar.activation(out=near[:], in_=dist[:], func=ACT.Exp, scale=-1.0)
+            a_banks[s] = bank
+            nears[s] = near
+
+        def back(s):
+            u, b, c0, width, slots = steps[s]
+            if slots[0] == 0:
+                h_rows[u] = held([P, PACK, width], BF16, "h_rows%d" % u)
+            for g, t in enumerate(slots):
+                cols = slice(g * width, (g + 1) * width)
+                nc.vector.scalar_tensor_tensor(
+                    out=h_rows[u][:, t, :], in0=a_banks[s][:, cols], scalar=gains[:, b, t : t + 1],
+                    in1=nears[s][:, cols], op0=ALU.mult, op1=ALU.mult,
+                )
+
+        def quantise_h(u):
+            b, c0, width = UNITS[u]
+            grouped = held([P, width, PACK], BF16, "h_bf%d" % u)
+            engine = nc.vector if u == len(UNITS) - 1 else nc.gpsimd
+            cast(engine, grouped[:], h_rows[u][:].rearrange("p t c -> p c t"))
+            h_q[u] = quantise("h%d" % u, grouped[:].rearrange("p c t -> p (c t)"), width)
+
+        def second_stage(u):
+            b, c0, width = UNITS[u]
+            half, cols = window(c0, width)
+            per_bank = BANK // width
+            for n0 in range(0, N // P, per_bank):
+                bank = psum.tile([P, BANK], F32, name="bank_by", tag="bank_by")
+                passes = []
+                for a in range(2):
+                    for g in range(per_bank):
+                        ncols = slice((n0 + g) * P, (n0 + g + 1) * P)
+                        passes.append((g, wd_w[:, a, ncols], wd_s[4 * a :, ncols], v_w[a, half][:, cols], v_s[half][4 * a :, cols]))
+                for blk, (hc, hs), hcols in ((0, h_q[half], cols), (1, h_q[u], slice(0, width))):
+                    for g in range(per_bank):
+                        ncols = slice((n0 + g) * P, (n0 + g + 1) * P)
+                        passes.append((g, wo_q[blk][0][:, ncols], wo_q[blk][1][:, ncols], hc[:, hcols], hs[:, hcols]))
+                for i, (g, lw, ls, rw, rs) in enumerate(passes):
+                    nc.tensor.matmul_mx(
+                        out=bank[:, g * width : (g + 1) * width],
+                        lhsT=lw.bitcast(FP8X4), lhsT_scale=ls, rhs=rw.bitcast(FP8X4), rhs_scale=rs,
+                        start=(i == 0), stop=(i == len(passes) - 1),
+                    )
+                result = ring.tile([P, per_bank, width], F32, name="result")
+                for g in range(per_bank):
+                    nc.scalar.activation(
+                        out=result[:, g, :], in_=bank[:, g * width : (g + 1) * width],
+                        func=ACT.Identity, bias=biases[:, n0 + g : n0 + g + 1],
+                    )
+                rows = out[n0 * P : (n0 + per_bank) * P, c0 : c0 + width]
+                nc.sync.dma_start(out=rows.rearrange("(g p) c -> p g c", p=P), in_=result[:])
+
+        LAG = 2
+        for s in range(len(steps) + LAG):
+            if s < len(steps):
+                front(s)
+            done = s - LAG
+            if done >= 0:
+                back(done)
+                u, b, c0, width, slots = steps[done]
+                if slots[-1] == PACK - 1:
+                    quantise_h(u)
+                    if u < 2:
+                        prepare_wo(u)
+                    else:
+                        second_stage(u)
+            if s == 3:
+                prepare_wa_block1()

@@ -1,6 +1,7 @@
 from contextlib import ExitStack
 
 import concourse.mybir as mybir
+from concourse.masks import make_identity
 
 K, K2, H, N, T, S = 1024, 512, 1024, 512, 2048, 1024
 FLOPS = 2 * S * (K * H + K2 * H + H * N + K * N)
@@ -20,6 +21,7 @@ P = 128
 PACK = 4
 PASS = P * PACK
 BANK = 512
+RUN = 8
 UNITS = [(0, 0, 512), (0, 512, 512), (1, 0, 512), (1, 512, 256), (1, 768, 256)]
 
 
@@ -41,20 +43,21 @@ def tile_list_anaesthesia_depth_agreement_kernel(
         tab_s = held([P, T], U8, "tab_s")
         wb_raw_w = held([P, 2 * H], U8, "wb_raw_w")
         wb_rows_s = held([P, H], U8, "wb_rows_s")
-        wb_raw_s = held([P, H], U8, "wb_raw_s")
         wb_w = held([P, 2 * H], U8, "wb_w")
         wb_s = held([P, H], U8, "wb_s")
         xs_w = held([P, S], I32, "xs_w")
         xs_s = held([P, S], U8, "xs_s")
         wd_w = held([P, 2, N], I32, "wd_w")
         wd_s = held([P, N], U8, "wd_s")
-        gains = held([P, 2, PACK], F32, "gains")
-        biases = held([P, N // P], F32, "biases")
+        vector_rows = held([P, P], F32, "vector_rows")
+        identity = held([P, P], F32, "identity")
+        vectors = held([P, 2 * PACK + N // P], F32, "vectors")
         wa_raw = {(a, b): held([P, PACK, PASS], F32, "wa_raw%d%d" % (a, b)) for b in range(2) for a in range(2)}
         wo_raw = [held([P, PACK, N], F32, "wo_raw%d" % b) for b in range(2)]
 
-        nc.vector.memset(wb_raw_s[:].bitcast(I32), 0)
         nc.gpsimd.memset(tab_s[:].bitcast(I32), 0)
+        nc.gpsimd.memset(vector_rows[:], 0.0)
+        make_identity(nc, identity[:])
 
         def load_scale_quadrant(queue, plane, scales, q):
             passes = scales.shape[0]
@@ -74,44 +77,79 @@ def tile_list_anaesthesia_depth_agreement_kernel(
             rows = wa[a * PASS : (a + 1) * PASS, b * PASS : (b + 1) * PASS]
             nc.sync.dma_start(out=wa_raw[a, b][:], in_=rows.rearrange("(p j) c -> p j c", j=PACK))
 
-        nc.sync.dma_start(out=wb_raw_w[:].bitcast(I32), in_=wb_words[0].bitcast(I32))
         load_scale_quadrant(nc.scalar, wb_rows_s, wb_scales, 0)
-        load_words(xs_w[:], xs_words[0])
-        load_scale_quadrant(nc.scalar, wb_rows_s, wb_scales, 1)
-        load_words(tab_w[0][:], tab_words[0])
+        load_scale_quadrant(nc.sync, wb_rows_s, wb_scales, 1)
         load_scale_quadrant(nc.scalar, wb_rows_s, wb_scales, 2)
-        nc.sync.dma_start(offsets[:], offs)
-        load_scale_quadrant(nc.scalar, wb_rows_s, wb_scales, 3)
-        load_words(tab_w[1][:], tab_words[1])
+        load_scale_quadrant(nc.sync, wb_rows_s, wb_scales, 3)
         load_scale_quadrant(nc.scalar, xs_s, xs_scales, 0)
-        load_wa(0, 0)
+        nc.sync.dma_start(out=wb_raw_w[:].bitcast(I32), in_=wb_words[0].bitcast(I32))
         load_scale_quadrant(nc.scalar, xs_s, xs_scales, 1)
-        load_wa(1, 0)
+        load_words(tab_w[0][:], tab_words[0])
         load_scale_quadrant(nc.scalar, xs_s, xs_scales, 2)
-        nc.sync.dma_start(out=gains[:], in_=gain.rearrange("(b p t) -> p b t", p=P, t=PACK))
+        nc.sync.dma_start(offsets[:], offs)
         load_scale_quadrant(nc.scalar, xs_s, xs_scales, 3)
+        load_words(xs_w[:], xs_words[0])
+        load_wa(0, 0)
+        load_scale_rows(nc.sync, tab_s, tab_scales)
+        load_words(tab_w[1][:], tab_words[1])
+        load_wa(1, 0)
+        gain_rows = gain.rearrange("(b q t u) -> b t q u", b=2, t=PACK, u=RUN)
+        for b in range(2):
+            nc.sync.dma_start(
+                out=vector_rows[PACK * b : PACK * (b + 1), :].rearrange("t (q u) -> t q u", u=RUN), in_=gain_rows[b]
+            )
+        nc.sync.dma_start(out=vector_rows[2 * PACK : 2 * PACK + N // P, :], in_=bo.rearrange("(t p) -> t p", p=P))
         load_wa(0, 1)
         load_wa(1, 1)
         nc.sync.dma_start(out=wd_w[:], in_=wd_words.rearrange("a p c i -> p a (c i)").bitcast(I32))
         load_scale_rows(nc.sync, wd_s, wd_scales)
         for b in range(2):
-            rows = wo[b * PASS : (b + 1) * PASS, :]
-            nc.sync.dma_start(out=wo_raw[b][:], in_=rows.rearrange("(p j) c -> p j c", j=PACK))
-        with nc.allow_non_contiguous_dma(reason="one bias value a partition"):
-            nc.sync.dma_start(out=biases[:], in_=bo.rearrange("(t p) -> p t", p=P))
-        load_scale_rows(nc.gpsimd, tab_s, tab_scales)
+            rows = wo[b * PASS : (b + 1) * PASS, :].rearrange("(q t u) c -> t q u c", t=PACK, u=RUN)
+            for t in range(PACK):
+                nc.sync.dma_start(out=wo_raw[b][:, t, :], in_=rows[t])
 
         for q in range(4):
             rows = slice(32 * q, 32 * q + 4)
-            nc.vector.tensor_copy(out=wb_raw_s[rows, :].bitcast(I32), in_=wb_rows_s[rows, :].bitcast(I32))
+            nc.vector.tensor_copy(
+                out=wb_s[rows, :].bitcast(I32).rearrange("p (b t q w) -> p b t q w", b=2, t=PACK, w=RUN // 4),
+                in_=wb_rows_s[rows, :].bitcast(I32).rearrange("p (b q t w) -> p b t q w", b=2, t=PACK, w=RUN // 4),
+            )
         nc.vector.tensor_copy(
-            out=wb_w[:].bitcast(U16).rearrange("p (b t m) -> p b t m", b=2, t=PACK),
-            in_=wb_raw_w[:].bitcast(U16).rearrange("p (b m t) -> p b t m", b=2, t=PACK),
+            out=wb_w[:].bitcast(I32).rearrange("p (b t q w) -> p b t q w", b=2, t=PACK, w=RUN // 2),
+            in_=wb_raw_w[:].bitcast(I32).rearrange("p (b q t w) -> p b t q w", b=2, t=PACK, w=RUN // 2),
         )
-        nc.vector.tensor_copy(
-            out=wb_s[:].rearrange("p (b t m) -> p b t m", b=2, t=PACK),
-            in_=wb_raw_s[:].rearrange("p (b m t) -> p b t m", b=2, t=PACK),
-        )
+
+        def cast(engine, dst, src):
+            if engine is nc.gpsimd:
+                nc.gpsimd.tensor_scalar(dst, src, 1.0, 0.0, ALU.mult, ALU.add)
+            elif engine is nc.scalar:
+                nc.scalar.copy(out=dst, in_=src)
+            else:
+                nc.vector.tensor_copy(out=dst, in_=src)
+
+        wa_q = {}
+
+        wa_bf = {}
+
+        def round_wa(a, b, t, engine):
+            part = t // 2
+            if t % 2 == 0:
+                wa_bf[a, b, part] = held([P, 2, P, PACK], BF16, "wa_bf%d%d%d" % (a, b, part))
+            src = wa_raw[a, b][:].rearrange("p j (q t u) -> p t q u j", t=PACK, u=RUN)[:, t]
+            cast(engine, wa_bf[a, b, part][:, t % 2].rearrange("p (q u) j -> p q u j", u=RUN), src)
+
+        def quantise(name, grouped_flat, words):
+            codes = held([P, words], U32, name + "_w")
+            scales = held([P, words], U8, name + "_s")
+            nc.vector.quantize_mx(out=codes[:].bitcast(FP8X4), scales=scales[:], in_=grouped_flat)
+            return codes, scales
+
+        def quantise_wa(a, b, part):
+            grouped = wa_bf[a, b, part]
+            wa_q[a, b, part] = quantise("wa%d%d%d" % (a, b, part), grouped[:].rearrange("p t m j -> p (t m j)"), 2 * P)
+
+        for t in (2, 3):
+            round_wa(1, 0, t, nc.scalar)
 
         steps = []
         for u, (b, c0, width) in enumerate(UNITS):
@@ -150,51 +188,44 @@ def tile_list_anaesthesia_depth_agreement_kernel(
             part = offsets[:, 32 * half : 32 * (half + 1)]
             nc.vector.tensor_copy(v_s[half][:], tab_s[:].indirect(part))
 
-        def cast(engine, dst, src):
-            if engine is nc.gpsimd:
-                nc.gpsimd.tensor_scalar(dst, src, 1.0, 0.0, ALU.mult, ALU.add)
-            else:
-                nc.vector.tensor_copy(out=dst, in_=src)
-
-        wa_q = {}
-
-        def round_wa(a, b, part, engine):
-            grouped = held([P, 2, P, PACK], BF16, "wa_bf%d%d%d" % (a, b, part))
-            src = wa_raw[a, b][:].rearrange("p j (m t) -> p t m j", t=PACK)[:, 2 * part : 2 * part + 2]
-            cast(engine, grouped[:], src)
-            return grouped
-
-        def quantise(name, grouped_flat, words):
-            codes = held([P, words], U32, name + "_w")
-            scales = held([P, words], U8, name + "_s")
-            nc.vector.quantize_mx(out=codes[:].bitcast(FP8X4), scales=scales[:], in_=grouped_flat)
-            return codes, scales
-
-        def quantise_wa(a, b, part, grouped):
-            wa_q[a, b, part] = quantise("wa%d%d%d" % (a, b, part), grouped[:].rearrange("p t m j -> p (t m j)"), 2 * P)
-
-        for a in range(2):
-            for half in range(2):
-                gather_words(a, half)
+        for half in range(2):
+            gather_words(0, half)
         for half in range(2):
             gather_scales(half)
-        first = [round_wa(0, 0, part, nc.gpsimd) for part in range(2)]
-        second = [round_wa(1, 0, 0, nc.vector), round_wa(1, 0, 1, nc.gpsimd)]
+        for t in range(PACK):
+            round_wa(0, 0, t, nc.vector)
+        gather_words(1, 0)
         for part in range(2):
-            quantise_wa(0, 0, part, first[part])
-            quantise_wa(1, 0, part, second[part])
+            quantise_wa(0, 0, part)
+        for t in range(2):
+            round_wa(1, 0, t, nc.vector)
+        gather_words(1, 1)
+        for part in range(2):
+            quantise_wa(1, 0, part)
+
+        turned = psum.tile([P, BANK], F32, name="bank_a", tag="bank_a")
+        nc.tensor.transpose(turned[:, :P], vector_rows[:], identity[:])
+        nc.vector.tensor_copy(out=vectors[:], in_=turned[:, : 2 * PACK + N // P])
 
         wo_q = {}
 
-        def prepare_wa_block1():
-            for a in range(2):
-                for part in range(2):
-                    quantise_wa(a, 1, part, round_wa(a, 1, part, nc.gpsimd))
+        wo_bf = [held([P, N, PACK], BF16, "wo_bf%d" % b) for b in range(2)]
 
-        def prepare_wo(b):
-            grouped = held([P, N, PACK], BF16, "wo_bf%d" % b)
-            cast(nc.gpsimd, grouped[:], wo_raw[b][:].rearrange("p j c -> p c j"))
-            wo_q[b] = quantise("wo%d" % b, grouped[:].rearrange("p c j -> p (c j)"), N)
+        def round_wa_late(i):
+            part, a, t = i // 4, (i // 2) % 2, i % 2
+            round_wa(a, 1, 2 * part + t, nc.scalar)
+            if t == 1:
+                quantise_wa(a, 1, part)
+
+        def round_wo(i):
+            b, n = divmod(i, N // P)
+            cols = slice(n * P, (n + 1) * P)
+            cast(nc.scalar if b == 0 else nc.vector, wo_bf[b][:, cols, :], wo_raw[b][:, :, cols].rearrange("p j c -> p c j"))
+            if n == N // P - 1:
+                wo_q[b] = quantise("wo%d" % b, wo_bf[b][:].rearrange("p c j -> p (c j)"), N)
+
+        side_work = [(round_wa_late, i) for i in range(8)] + [(round_wo, i) for i in range(8)]
+        SIDE_STEPS = 12
 
         h_rows = {}
         h_q = {}
@@ -238,15 +269,14 @@ def tile_list_anaesthesia_depth_agreement_kernel(
             for g, t in enumerate(slots):
                 cols = slice(g * width, (g + 1) * width)
                 nc.vector.scalar_tensor_tensor(
-                    out=h_rows[u][:, t, :], in0=a_banks[s][:, cols], scalar=gains[:, b, t : t + 1],
+                    out=h_rows[u][:, t, :], in0=a_banks[s][:, cols], scalar=vectors[:, PACK * b + t : PACK * b + t + 1],
                     in1=nears[s][:, cols], op0=ALU.mult, op1=ALU.mult,
                 )
 
         def quantise_h(u):
             b, c0, width = UNITS[u]
             grouped = held([P, width, PACK], BF16, "h_bf%d" % u)
-            engine = nc.vector if u == len(UNITS) - 1 else nc.gpsimd
-            cast(engine, grouped[:], h_rows[u][:].rearrange("p t c -> p c t"))
+            cast(nc.vector, grouped[:], h_rows[u][:].rearrange("p t c -> p c t"))
             h_q[u] = quantise("h%d" % u, grouped[:].rearrange("p c t -> p (c t)"), width)
 
         def second_stage(u):
@@ -272,10 +302,12 @@ def tile_list_anaesthesia_depth_agreement_kernel(
                     )
                 result = ring.tile([P, per_bank, width], F32, name="result")
                 for g in range(per_bank):
-                    nc.scalar.activation(
-                        out=result[:, g, :], in_=bank[:, g * width : (g + 1) * width],
-                        func=ACT.Identity, bias=biases[:, n0 + g : n0 + g + 1],
-                    )
+                    bias = vectors[:, 2 * PACK + n0 + g : 2 * PACK + n0 + g + 1]
+                    sums = bank[:, g * width : (g + 1) * width]
+                    if u == len(UNITS) - 1 and n0 > 0:
+                        nc.vector.tensor_scalar(result[:, g, :], sums, bias, None, ALU.add)
+                    else:
+                        nc.scalar.activation(out=result[:, g, :], in_=sums, func=ACT.Identity, bias=bias)
                 rows = out[n0 * P : (n0 + per_bank) * P, c0 : c0 + width]
                 nc.sync.dma_start(out=rows.rearrange("(g p) c -> p g c", p=P), in_=result[:])
 
@@ -289,9 +321,9 @@ def tile_list_anaesthesia_depth_agreement_kernel(
                 u, b, c0, width, slots = steps[done]
                 if slots[-1] == PACK - 1:
                     quantise_h(u)
-                    if u < 2:
-                        prepare_wo(u)
-                    else:
+                    if u >= 2:
                         second_stage(u)
-            if s == 3:
-                prepare_wa_block1()
+            if 1 <= s <= SIDE_STEPS:
+                lo, hi = (s - 1) * len(side_work) // SIDE_STEPS, s * len(side_work) // SIDE_STEPS
+                for work, i in side_work[lo:hi]:
+                    work(i)

@@ -20,9 +20,23 @@ ACT = mybir.ActivationFunctionType
 P = 128
 PACK = 4
 PASS = P * PACK
-BANK = 512
 RUN = 8
-UNITS = [(0, 0, 512), (0, 512, 512), (1, 0, 512), (1, 512, 256), (1, 768, 256)]
+BANK = 512
+HALF = S // 2
+N_TILES = N // P
+QUADRANTS = 4
+
+UNITS = [(0, 0, 512), (0, 512, 512)] + [(1, c0, 256) for c0 in range(0, S, 256)]
+STEPS = [
+    (u, list(range(t0, t0 + BANK // width)))
+    for u, (b, c0, width) in enumerate(UNITS)
+    for t0 in range(0, PACK, BANK // width)
+]
+EXP_LAG = 1
+PRODUCT_LAG = 3
+ROUND_STEPS = 10
+FIRST_BANKS = 6
+RING = 4
 
 
 def tile_list_anaesthesia_depth_agreement_kernel(
@@ -32,17 +46,23 @@ def tile_list_anaesthesia_depth_agreement_kernel(
     nc = tc.nc
     with ExitStack() as ctx:
         keep = ctx.enter_context(tc.tile_pool(name="keep", bufs=1))
-        ring = ctx.enter_context(tc.tile_pool(name="ring", bufs=4))
-        psum = ctx.enter_context(tc.psum_pool(name="psum", bufs=4))
+        ring = ctx.enter_context(tc.tile_pool(name="ring", bufs=RING))
+        psum = ctx.enter_context(tc.psum_pool(name="psum", bufs=1))
 
         def held(shape, dtype, name):
             return keep.tile(shape, dtype, name=name, align_bytes=64)
 
+        def first_bank():
+            return psum.tile([P, BANK], F32, name="first_bank", bufs=FIRST_BANKS)
+
+        def out_bank():
+            return psum.tile([P, BANK], F32, name="out_bank", bufs=8 - FIRST_BANKS)
+
         offsets = held([P, S // 16], U16, "offsets")
         tab_w = [held([P, T], I32, "tab_w%d" % a) for a in range(2)]
         tab_s = held([P, T], U8, "tab_s")
-        wb_raw_w = held([P, 2 * H], U8, "wb_raw_w")
-        wb_rows_s = held([P, H], U8, "wb_rows_s")
+        wb_loaded_w = held([P, 2 * H], U8, "wb_loaded_w")
+        wb_loaded_s = held([P, H], U8, "wb_loaded_s")
         wb_w = held([P, 2 * H], U8, "wb_w")
         wb_s = held([P, H], U8, "wb_s")
         xs_w = held([P, S], I32, "xs_w")
@@ -51,75 +71,70 @@ def tile_list_anaesthesia_depth_agreement_kernel(
         wd_s = held([P, N], U8, "wd_s")
         vector_rows = held([P, P], F32, "vector_rows")
         identity = held([P, P], F32, "identity")
-        vectors = held([P, 2 * PACK + N // P], F32, "vectors")
-        wa_raw = {(a, b): held([P, PACK, PASS], F32, "wa_raw%d%d" % (a, b)) for b in range(2) for a in range(2)}
-        wo_raw = [held([P, PACK, N], F32, "wo_raw%d" % b) for b in range(2)]
+        vectors = held([P, 2 * PACK + N_TILES], F32, "vectors")
+        wa_loaded = {(a, b): held([P, PACK, PASS], F32, "wa_loaded%d%d" % (a, b)) for b in range(2) for a in range(2)}
+        wo_loaded = [held([P, PACK, N], F32, "wo_loaded%d" % b) for b in range(2)]
 
         nc.gpsimd.memset(tab_s[:].bitcast(I32), 0)
         nc.gpsimd.memset(vector_rows[:], 0.0)
         make_identity(nc, identity[:])
 
-        def load_scale_quadrant(queue, plane, scales, q):
-            passes = scales.shape[0]
+        def load_scales(queue, tile, scales, quadrant):
+            rows = 4 * scales.shape[0]
             queue.dma_start(
-                out=plane[32 * q : 32 * q + 4 * passes, :].bitcast(I32),
-                in_=scales[:, 4 * q : 4 * q + 4, :].bitcast(I32),
+                out=tile[32 * quadrant : 32 * quadrant + rows, :].bitcast(I32),
+                in_=scales[:, 4 * quadrant : 4 * quadrant + 4, :].bitcast(I32),
             )
 
-        def load_scale_rows(queue, plane, scales):
-            for q in range(4):
-                load_scale_quadrant(queue, plane, scales, q)
-
         def load_words(tile, words):
-            nc.sync.dma_start(out=tile, in_=words.rearrange("p c i -> p (c i)").bitcast(I32))
+            nc.sync.dma_start(out=tile[:], in_=words.rearrange("p c i -> p (c i)").bitcast(I32))
 
         def load_wa(a, b):
             rows = wa[a * PASS : (a + 1) * PASS, b * PASS : (b + 1) * PASS]
-            nc.sync.dma_start(out=wa_raw[a, b][:], in_=rows.rearrange("(p j) c -> p j c", j=PACK))
+            nc.sync.dma_start(out=wa_loaded[a, b][:], in_=rows.rearrange("(p i) c -> p i c", i=PACK))
 
-        load_scale_quadrant(nc.scalar, wb_rows_s, wb_scales, 0)
-        load_scale_quadrant(nc.sync, wb_rows_s, wb_scales, 1)
-        load_scale_quadrant(nc.scalar, wb_rows_s, wb_scales, 2)
-        load_scale_quadrant(nc.sync, wb_rows_s, wb_scales, 3)
-        load_scale_quadrant(nc.scalar, xs_s, xs_scales, 0)
-        nc.sync.dma_start(out=wb_raw_w[:].bitcast(I32), in_=wb_words[0].bitcast(I32))
-        load_scale_quadrant(nc.scalar, xs_s, xs_scales, 1)
-        load_words(tab_w[0][:], tab_words[0])
-        load_scale_quadrant(nc.scalar, xs_s, xs_scales, 2)
+        for quadrant in range(QUADRANTS):
+            load_scales(nc.sync if quadrant % 2 else nc.scalar, wb_loaded_s, wb_scales, quadrant)
+        load_scales(nc.scalar, xs_s, xs_scales, 0)
+        nc.sync.dma_start(out=wb_loaded_w[:].bitcast(I32), in_=wb_words[0].bitcast(I32))
+        load_scales(nc.scalar, xs_s, xs_scales, 1)
+        load_words(tab_w[0], tab_words[0])
+        load_scales(nc.scalar, xs_s, xs_scales, 2)
         nc.sync.dma_start(offsets[:], offs)
-        load_scale_quadrant(nc.scalar, xs_s, xs_scales, 3)
-        load_words(xs_w[:], xs_words[0])
+        load_scales(nc.scalar, xs_s, xs_scales, 3)
+        load_words(xs_w, xs_words[0])
+        for quadrant in range(QUADRANTS):
+            load_scales(nc.sync, tab_s, tab_scales, quadrant)
         load_wa(0, 0)
-        load_scale_rows(nc.sync, tab_s, tab_scales)
-        load_words(tab_w[1][:], tab_words[1])
+        load_words(tab_w[1], tab_words[1])
         load_wa(1, 0)
         gain_rows = gain.rearrange("(b q t u) -> b t q u", b=2, t=PACK, u=RUN)
         for b in range(2):
-            nc.sync.dma_start(
-                out=vector_rows[PACK * b : PACK * (b + 1), :].rearrange("t (q u) -> t q u", u=RUN), in_=gain_rows[b]
-            )
-        nc.sync.dma_start(out=vector_rows[2 * PACK : 2 * PACK + N // P, :], in_=bo.rearrange("(t p) -> t p", p=P))
-        load_wa(0, 1)
-        load_wa(1, 1)
-        nc.sync.dma_start(out=wd_w[:], in_=wd_words.rearrange("a p c i -> p a (c i)").bitcast(I32))
-        load_scale_rows(nc.sync, wd_s, wd_scales)
+            rows = vector_rows[PACK * b : PACK * (b + 1), :]
+            nc.sync.dma_start(out=rows.rearrange("t (q u) -> t q u", u=RUN), in_=gain_rows[b])
+        nc.sync.dma_start(out=vector_rows[2 * PACK : 2 * PACK + N_TILES, :], in_=bo.rearrange("(n p) -> n p", p=P))
+        for a in range(2):
+            load_wa(a, 1)
         for b in range(2):
-            rows = wo[b * PASS : (b + 1) * PASS, :].rearrange("(q t u) c -> t q u c", t=PACK, u=RUN)
+            slot_rows = wo[b * PASS : (b + 1) * PASS, :].rearrange("(q t u) c -> t q u c", t=PACK, u=RUN)
             for t in range(PACK):
-                nc.sync.dma_start(out=wo_raw[b][:, t, :], in_=rows[t])
+                nc.sync.dma_start(out=wo_loaded[b][:, t, :], in_=slot_rows[t])
+        nc.sync.dma_start(out=wd_w[:], in_=wd_words.rearrange("a p c i -> p a (c i)").bitcast(I32))
+        for quadrant in range(QUADRANTS):
+            load_scales(nc.sync, wd_s, wd_scales, quadrant)
 
-        for q in range(4):
-            rows = slice(32 * q, 32 * q + 4)
+        for quadrant in range(QUADRANTS):
+            rows = slice(32 * quadrant, 32 * quadrant + 4)
             nc.vector.tensor_copy(
                 out=wb_s[rows, :].bitcast(I32).rearrange("p (b t q w) -> p b t q w", b=2, t=PACK, w=RUN // 4),
-                in_=wb_rows_s[rows, :].bitcast(I32).rearrange("p (b q t w) -> p b t q w", b=2, t=PACK, w=RUN // 4),
+                in_=wb_loaded_s[rows, :].bitcast(I32).rearrange("p (b q t w) -> p b t q w", b=2, t=PACK, w=RUN // 4),
             )
         nc.vector.tensor_copy(
             out=wb_w[:].bitcast(I32).rearrange("p (b t q w) -> p b t q w", b=2, t=PACK, w=RUN // 2),
-            in_=wb_raw_w[:].bitcast(I32).rearrange("p (b q t w) -> p b t q w", b=2, t=PACK, w=RUN // 2),
+            in_=wb_loaded_w[:].bitcast(I32).rearrange("p (b q t w) -> p b t q w", b=2, t=PACK, w=RUN // 2),
         )
 
-        def cast(engine, dst, src):
+        def interleave(engine, dst, src):
             if engine is nc.gpsimd:
                 nc.gpsimd.tensor_scalar(dst, src, 1.0, 0.0, ALU.mult, ALU.add)
             elif engine is nc.scalar:
@@ -127,39 +142,33 @@ def tile_list_anaesthesia_depth_agreement_kernel(
             else:
                 nc.vector.tensor_copy(out=dst, in_=src)
 
-        wa_q = {}
-
-        wa_bf = {}
-
-        def round_wa(a, b, t, engine):
-            part = t // 2
-            if t % 2 == 0:
-                wa_bf[a, b, part] = held([P, 2, P, PACK], BF16, "wa_bf%d%d%d" % (a, b, part))
-            src = wa_raw[a, b][:].rearrange("p j (q t u) -> p t q u j", t=PACK, u=RUN)[:, t]
-            cast(engine, wa_bf[a, b, part][:, t % 2].rearrange("p (q u) j -> p q u j", u=RUN), src)
-
-        def quantise(name, grouped_flat, words):
-            codes = held([P, words], U32, name + "_w")
-            scales = held([P, words], U8, name + "_s")
-            nc.vector.quantize_mx(out=codes[:].bitcast(FP8X4), scales=scales[:], in_=grouped_flat)
+        def quantise(name, values, columns):
+            codes = held([P, columns], U32, name + "_codes")
+            scales = held([P, columns], U8, name + "_scales")
+            nc.vector.quantize_mx(out=codes[:].bitcast(FP8X4), scales=scales[:], in_=values)
             return codes, scales
 
-        def quantise_wa(a, b, part):
-            grouped = wa_bf[a, b, part]
-            wa_q[a, b, part] = quantise("wa%d%d%d" % (a, b, part), grouped[:].rearrange("p t m j -> p (t m j)"), 2 * P)
+        wa_bf = {
+            (a, b, pair): held([P, 2, P, PACK], BF16, "wa_bf%d%d%d" % (a, b, pair))
+            for a in range(2) for b in range(2) for pair in range(2)
+        }
+        wa_mx = {}
+
+        def round_wa(a, b, t, engine):
+            src = wa_loaded[a, b][:].rearrange("p i (q t u) -> p t q u i", t=PACK, u=RUN)[:, t]
+            interleave(engine, wa_bf[a, b, t // 2][:, t % 2].rearrange("p (q u) i -> p q u i", u=RUN), src)
+
+        def quantise_wa(a, b, pair):
+            values = wa_bf[a, b, pair][:].rearrange("p t m i -> p (t m i)")
+            wa_mx[a, b, pair] = quantise("wa%d%d%d" % (a, b, pair), values, 2 * P)
 
         for t in (2, 3):
             round_wa(1, 0, t, nc.scalar)
 
-        steps = []
-        for u, (b, c0, width) in enumerate(UNITS):
-            per_bank = BANK // width
-            for t0 in range(0, PACK, per_bank):
-                steps.append((u, b, c0, width, list(range(t0, t0 + per_bank))))
-
-        b_sb = []
-        for s, (u, b, c0, width, slots) in enumerate(steps):
-            bank = psum.tile([P, BANK], F32, name="bank_by", tag="bank_by")
+        b_kept = []
+        for s, (u, slots) in enumerate(STEPS):
+            b, c0, width = UNITS[u]
+            bank = first_bank()
             for g, t in enumerate(slots):
                 col = b * PASS + t * P
                 nc.tensor.matmul_mx(
@@ -171,159 +180,172 @@ def tile_list_anaesthesia_depth_agreement_kernel(
                     start=True,
                     stop=True,
                 )
-            kept = held([P, BANK], F32, "b_sb%d" % s)
+            kept = held([P, BANK], F32, "b_kept%d" % s)
             nc.scalar.activation(out=kept[:], in_=bank[:], func=ACT.Copy)
-            b_sb.append(kept)
+            b_kept.append(kept)
 
-        v_w = {}
-        v_s = {}
+        v_w = {(a, half): held([P, HALF], U32, "v_w%d%d" % (a, half)) for a in range(2) for half in range(2)}
+        v_s = [held([P, HALF], U8, "v_s%d" % half) for half in range(2)]
+
+        def list_half(half):
+            return offsets[:, half * HALF // 16 : (half + 1) * HALF // 16]
 
         def gather_words(a, half):
-            v_w[a, half] = held([P, BANK], U32, "v_w%d%d" % (a, half))
-            part = offsets[:, 32 * half : 32 * (half + 1)]
-            nc.vector.tensor_copy(v_w[a, half][:], tab_w[a][:].bitcast(U32).indirect(part))
+            nc.vector.tensor_copy(v_w[a, half][:], tab_w[a][:].bitcast(U32).indirect(list_half(half)))
 
         def gather_scales(half):
-            v_s[half] = held([P, BANK], U8, "v_s%d" % half)
-            part = offsets[:, 32 * half : 32 * (half + 1)]
-            nc.vector.tensor_copy(v_s[half][:], tab_s[:].indirect(part))
+            nc.vector.tensor_copy(v_s[half][:], tab_s[:].indirect(list_half(half)))
+
+        def looked_up(a, c0, width):
+            half, lo = divmod(c0, HALF)
+            return v_w[a, half][:, lo : lo + width], v_s[half][4 * a :, lo : lo + width]
 
         for half in range(2):
             gather_words(0, half)
-        for half in range(2):
-            gather_scales(half)
+        gather_scales(0)
         for t in range(PACK):
             round_wa(0, 0, t, nc.vector)
+        gather_scales(1)
+        for pair in range(2):
+            quantise_wa(0, 0, pair)
         gather_words(1, 0)
-        for part in range(2):
-            quantise_wa(0, 0, part)
-        for t in range(2):
+        for t in (0, 1):
             round_wa(1, 0, t, nc.vector)
+        quantise_wa(1, 0, 0)
         gather_words(1, 1)
-        for part in range(2):
-            quantise_wa(1, 0, part)
+        quantise_wa(1, 0, 1)
 
-        turned = psum.tile([P, BANK], F32, name="bank_a", tag="bank_a")
+        turned = first_bank()
         nc.tensor.transpose(turned[:, :P], vector_rows[:], identity[:])
-        nc.vector.tensor_copy(out=vectors[:], in_=turned[:, : 2 * PACK + N // P])
-
-        wo_q = {}
+        nc.scalar.copy(out=vectors[:], in_=turned[:, : 2 * PACK + N_TILES])
 
         wo_bf = [held([P, N, PACK], BF16, "wo_bf%d" % b) for b in range(2)]
+        wo_mx = {}
 
-        def round_wa_late(i):
-            part, a, t = i // 4, (i // 2) % 2, i % 2
-            round_wa(a, 1, 2 * part + t, nc.scalar)
-            if t == 1:
-                quantise_wa(a, 1, part)
+        def round_late_wa(a, t):
+            round_wa(a, 1, t, nc.gpsimd)
+            if t % 2 == 1:
+                quantise_wa(a, 1, t // 2)
 
-        def round_wo(i):
-            b, n = divmod(i, N // P)
+        def round_wo(b, n):
             cols = slice(n * P, (n + 1) * P)
-            cast(nc.scalar if b == 0 else nc.vector, wo_bf[b][:, cols, :], wo_raw[b][:, :, cols].rearrange("p j c -> p c j"))
-            if n == N // P - 1:
-                wo_q[b] = quantise("wo%d" % b, wo_bf[b][:].rearrange("p c j -> p (c j)"), N)
+            engine = nc.gpsimd if b == 1 else nc.scalar
+            interleave(engine, wo_bf[b][:, cols, :], wo_loaded[b][:, :, cols].rearrange("p t c -> p c t"))
+            if n == N_TILES - 1:
+                wo_mx[b] = quantise("wo%d" % b, wo_bf[b][:].rearrange("p c t -> p (c t)"), N)
 
-        side_work = [(round_wa_late, i) for i in range(8)] + [(round_wo, i) for i in range(8)]
-        SIDE_STEPS = 12
+        late_pieces = [(round_late_wa, a, t) for a in range(2) for t in range(PACK)]
+        late_pieces.extend([(round_wo, b, n) for b in range(2) for n in range(N_TILES)])
 
-        h_rows = {}
-        h_q = {}
-        a_banks = {}
-        nears = {}
+        a_banks, distances, nears, h_slots, h_mx = {}, {}, {}, {}, {}
 
-        def window(c0, width):
-            half, lo = divmod(c0, BANK)
-            return half, slice(lo, lo + width)
-
-        def front(s):
-            u, b, c0, width, slots = steps[s]
-            half, cols = window(c0, width)
-            bank = psum.tile([P, BANK], F32, name="bank_a", tag="bank_a")
+        def difference(s):
+            u, slots = STEPS[s]
+            b, c0, width = UNITS[u]
+            bank = first_bank()
             for g, t in enumerate(slots):
-                part, m0 = t // 2, (t % 2) * P
+                cols = slice((t % 2) * P, (t % 2 + 1) * P)
                 for a in range(2):
-                    codes, scales = wa_q[a, b, part]
+                    codes, scales = wa_mx[a, b, t // 2]
+                    words, word_scales = looked_up(a, c0, width)
                     nc.tensor.matmul_mx(
                         out=bank[:, g * width : (g + 1) * width],
-                        lhsT=codes[:, m0 : m0 + P].bitcast(FP8X4),
-                        lhsT_scale=scales[:, m0 : m0 + P],
-                        rhs=v_w[a, half][:, cols].bitcast(FP8X4),
-                        rhs_scale=v_s[half][4 * a :, cols],
+                        lhsT=codes[:, cols].bitcast(FP8X4),
+                        lhsT_scale=scales[:, cols],
+                        rhs=words.bitcast(FP8X4),
+                        rhs_scale=word_scales,
                         start=(a == 0),
                         stop=(a == 1),
                     )
             diff = ring.tile([P, BANK], F32, name="diff")
-            nc.vector.tensor_tensor(diff[:], bank[:], b_sb[s][:], ALU.subtract)
-            dist = ring.tile([P, BANK], F32, name="dist")
-            nc.scalar.activation(out=dist[:], in_=diff[:], func=ACT.Abs)
-            near = ring.tile([P, BANK], F32, name="near")
-            nc.scalar.activation(out=near[:], in_=dist[:], func=ACT.Exp, scale=-1.0)
+            nc.vector.tensor_tensor(diff[:], bank[:], b_kept[s][:], ALU.subtract)
+            distance = ring.tile([P, BANK], F32, name="distance")
+            nc.scalar.activation(out=distance[:], in_=diff[:], func=ACT.Abs)
             a_banks[s] = bank
+            distances[s] = distance
+
+        def nearness(s):
+            near = ring.tile([P, BANK], F32, name="near")
+            nc.scalar.activation(out=near[:], in_=distances[s][:], func=ACT.Exp, scale=-1.0)
             nears[s] = near
 
-        def back(s):
-            u, b, c0, width, slots = steps[s]
+        def product(s):
+            u, slots = STEPS[s]
+            b, c0, width = UNITS[u]
             if slots[0] == 0:
-                h_rows[u] = held([P, PACK, width], BF16, "h_rows%d" % u)
+                h_slots[u] = held([P, PACK, width], BF16, "h_slots%d" % u)
             for g, t in enumerate(slots):
                 cols = slice(g * width, (g + 1) * width)
                 nc.vector.scalar_tensor_tensor(
-                    out=h_rows[u][:, t, :], in0=a_banks[s][:, cols], scalar=vectors[:, PACK * b + t : PACK * b + t + 1],
-                    in1=nears[s][:, cols], op0=ALU.mult, op1=ALU.mult,
+                    out=h_slots[u][:, t, :],
+                    in0=a_banks[s][:, cols],
+                    scalar=vectors[:, PACK * b + t : PACK * b + t + 1],
+                    in1=nears[s][:, cols],
+                    op0=ALU.mult,
+                    op1=ALU.mult,
                 )
 
         def quantise_h(u):
-            b, c0, width = UNITS[u]
-            grouped = held([P, width, PACK], BF16, "h_bf%d" % u)
-            cast(nc.vector, grouped[:], h_rows[u][:].rearrange("p t c -> p c t"))
-            h_q[u] = quantise("h%d" % u, grouped[:].rearrange("p c t -> p (c t)"), width)
+            width = UNITS[u][2]
+            h_bf = held([P, width, PACK], BF16, "h_bf%d" % u)
+            engine, piece = (nc.vector, width) if u == len(UNITS) - 1 else (nc.gpsimd, P)
+            for lo in range(0, width, piece):
+                src = h_slots[u][:, :, lo : lo + piece].rearrange("p t c -> p c t")
+                interleave(engine, h_bf[:, lo : lo + piece, :], src)
+            h_mx[u] = quantise("h%d" % u, h_bf[:].rearrange("p c t -> p (c t)"), width)
 
         def second_stage(u):
             b, c0, width = UNITS[u]
-            half, cols = window(c0, width)
+            half, lo = divmod(c0, HALF)
+            late = u >= len(UNITS) - 2
+            h_parts = [(h_mx[half], slice(lo, lo + width)), (h_mx[u], slice(0, width))]
             per_bank = BANK // width
-            for n0 in range(0, N // P, per_bank):
-                bank = psum.tile([P, BANK], F32, name="bank_by", tag="bank_by")
+            for n0 in range(0, N_TILES, per_bank):
+                bank = first_bank() if late else out_bank()
+                rows = [slice((n0 + g) * P, (n0 + g + 1) * P) for g in range(per_bank)]
                 passes = []
                 for a in range(2):
+                    words, word_scales = looked_up(a, c0, width)
                     for g in range(per_bank):
-                        ncols = slice((n0 + g) * P, (n0 + g + 1) * P)
-                        passes.append((g, wd_w[:, a, ncols], wd_s[4 * a :, ncols], v_w[a, half][:, cols], v_s[half][4 * a :, cols]))
-                for blk, (hc, hs), hcols in ((0, h_q[half], cols), (1, h_q[u], slice(0, width))):
+                        passes.append((g, wd_w[:, a, rows[g]], wd_s[4 * a :, rows[g]], words, word_scales))
+                for r_pass, ((codes, scales), cols) in enumerate(h_parts):
+                    wo_codes, wo_scales = wo_mx[r_pass]
                     for g in range(per_bank):
-                        ncols = slice((n0 + g) * P, (n0 + g + 1) * P)
-                        passes.append((g, wo_q[blk][0][:, ncols], wo_q[blk][1][:, ncols], hc[:, hcols], hs[:, hcols]))
-                for i, (g, lw, ls, rw, rs) in enumerate(passes):
+                        passes.append((g, wo_codes[:, rows[g]], wo_scales[:, rows[g]], codes[:, cols], scales[:, cols]))
+                for i, (g, weights, weight_scales, moving, moving_scales) in enumerate(passes):
                     nc.tensor.matmul_mx(
                         out=bank[:, g * width : (g + 1) * width],
-                        lhsT=lw.bitcast(FP8X4), lhsT_scale=ls, rhs=rw.bitcast(FP8X4), rhs_scale=rs,
-                        start=(i == 0), stop=(i == len(passes) - 1),
+                        lhsT=weights.bitcast(FP8X4),
+                        lhsT_scale=weight_scales,
+                        rhs=moving.bitcast(FP8X4),
+                        rhs_scale=moving_scales,
+                        start=(i == 0),
+                        stop=(i == len(passes) - 1),
                     )
                 result = ring.tile([P, per_bank, width], F32, name="result")
                 for g in range(per_bank):
                     bias = vectors[:, 2 * PACK + n0 + g : 2 * PACK + n0 + g + 1]
                     sums = bank[:, g * width : (g + 1) * width]
-                    if u == len(UNITS) - 1 and n0 > 0:
+                    if late and n0 > 0:
                         nc.vector.tensor_scalar(result[:, g, :], sums, bias, None, ALU.add)
                     else:
                         nc.scalar.activation(out=result[:, g, :], in_=sums, func=ACT.Identity, bias=bias)
-                rows = out[n0 * P : (n0 + per_bank) * P, c0 : c0 + width]
-                nc.sync.dma_start(out=rows.rearrange("(g p) c -> p g c", p=P), in_=result[:])
+                stored = out[n0 * P : (n0 + per_bank) * P, c0 : c0 + width]
+                nc.sync.dma_start(out=stored.rearrange("(g p) c -> p g c", p=P), in_=result[:])
 
-        LAG = 2
-        for s in range(len(steps) + LAG):
-            if s < len(steps):
-                front(s)
-            done = s - LAG
-            if done >= 0:
-                back(done)
-                u, b, c0, width, slots = steps[done]
+        for s in range(len(STEPS) + PRODUCT_LAG):
+            if s < len(STEPS):
+                difference(s)
+            if 0 <= s - EXP_LAG < len(STEPS):
+                nearness(s - EXP_LAG)
+            if s >= PRODUCT_LAG:
+                product(s - PRODUCT_LAG)
+                u, slots = STEPS[s - PRODUCT_LAG]
                 if slots[-1] == PACK - 1:
                     quantise_h(u)
-                    if u >= 2:
+                    if UNITS[u][0] == 1:
                         second_stage(u)
-            if 1 <= s <= SIDE_STEPS:
-                lo, hi = (s - 1) * len(side_work) // SIDE_STEPS, s * len(side_work) // SIDE_STEPS
-                for work, i in side_work[lo:hi]:
-                    work(i)
+            if 1 <= s <= ROUND_STEPS:
+                lo, hi = ((s - 1) * len(late_pieces) // ROUND_STEPS, s * len(late_pieces) // ROUND_STEPS)
+                for work, first, second in late_pieces[lo:hi]:
+                    work(first, second)

@@ -35,7 +35,8 @@ STEPS = [
 EXP_LAG = 1
 PRODUCT_LAG = 3
 ROUND_STEPS = 10
-FIRST_BANKS = 6
+FIRST_BANKS = 5
+OUT_BANKS = 2
 RING = 4
 
 
@@ -56,7 +57,7 @@ def tile_list_anaesthesia_depth_agreement_kernel(
             return psum.tile([P, BANK], F32, name="first_bank", bufs=FIRST_BANKS)
 
         def out_bank():
-            return psum.tile([P, BANK], F32, name="out_bank", bufs=8 - FIRST_BANKS)
+            return psum.tile([P, BANK], F32, name="out_bank", bufs=OUT_BANKS)
 
         offsets = held([P, S // 16], U16, "offsets")
         tab_w = [held([P, T], I32, "tab_w%d" % a) for a in range(2)]
@@ -71,7 +72,7 @@ def tile_list_anaesthesia_depth_agreement_kernel(
         wd_s = held([P, N], U8, "wd_s")
         vector_rows = held([P, P], F32, "vector_rows")
         identity = held([P, P], F32, "identity")
-        vectors = held([P, 2 * PACK + N_TILES], F32, "vectors")
+        biases = held([P, N_TILES], F32, "biases")
         wa_loaded = {(a, b): held([P, PACK, PASS], F32, "wa_loaded%d%d" % (a, b)) for b in range(2) for a in range(2)}
         wo_loaded = [held([P, PACK, N], F32, "wo_loaded%d" % b) for b in range(2)]
 
@@ -215,9 +216,9 @@ def tile_list_anaesthesia_depth_agreement_kernel(
         gather_words(1, 1)
         quantise_wa(1, 0, 1)
 
-        turned = first_bank()
-        nc.tensor.transpose(turned[:, :P], vector_rows[:], identity[:])
-        nc.scalar.copy(out=vectors[:], in_=turned[:, : 2 * PACK + N_TILES])
+        vectors = psum.tile([P, P], F32, name="vectors")
+        nc.tensor.transpose(vectors[:], vector_rows[:], identity[:])
+        nc.vector.tensor_copy(out=biases[:], in_=vectors[:, 2 * PACK : 2 * PACK + N_TILES])
 
         wo_bf = [held([P, N, PACK], BF16, "wo_bf%d" % b) for b in range(2)]
         wo_mx = {}
@@ -324,7 +325,7 @@ def tile_list_anaesthesia_depth_agreement_kernel(
                     )
                 result = ring.tile([P, per_bank, width], F32, name="result")
                 for g in range(per_bank):
-                    bias = vectors[:, 2 * PACK + n0 + g : 2 * PACK + n0 + g + 1]
+                    bias = biases[:, n0 + g : n0 + g + 1]
                     sums = bank[:, g * width : (g + 1) * width]
                     if late and n0 > 0:
                         nc.vector.tensor_scalar(result[:, g, :], sums, bias, None, ALU.add)

@@ -259,7 +259,7 @@ def tile_list_anaesthesia_depth_agreement_kernel(
                         stop=(a == 1),
                     )
             diff = ring.tile([P, BANK], F32, name="diff")
-            nc.vector.tensor_tensor(diff[:], bank[:], b_kept[s][:], ALU.subtract)
+            nc.vector.tensor_tensor(diff[:], b_kept[s][:], bank[:], ALU.subtract)
             distance = ring.tile([P, BANK], F32, name="distance")
             nc.scalar.activation(out=distance[:], in_=diff[:], func=ACT.Abs)
             a_banks[s] = bank
@@ -279,9 +279,9 @@ def tile_list_anaesthesia_depth_agreement_kernel(
                 cols = slice(g * width, (g + 1) * width)
                 nc.vector.scalar_tensor_tensor(
                     out=h_slots[u][:, t, :],
-                    in0=a_banks[s][:, cols],
+                    in0=nears[s][:, cols],
                     scalar=vectors[:, PACK * b + t : PACK * b + t + 1],
-                    in1=nears[s][:, cols],
+                    in1=a_banks[s][:, cols],
                     op0=ALU.mult,
                     op1=ALU.mult,
                 )

from contextlib import ExitStack

import concourse.mybir as mybir
from concourse.masks import make_identity

K, K2, H, N, T, S = 1024, 512, 1024, 512, 2048, 1024
FLOPS = 2 * S * (K * H + K2 * H + H * N + K * N)

F32 = mybir.dt.float32
BF16 = mybir.dt.bfloat16
I32 = mybir.dt.int32
U32 = mybir.dt.uint32
U16 = mybir.dt.uint16
U8 = mybir.dt.uint8
FP8X4 = mybir.dt.float8_e4m3fn_x4
FP4X4 = mybir.dt.float4_e2m1fn_x4
ALU = mybir.AluOpType
ACT = mybir.ActivationFunctionType

P = 128
PACK = 4
PASS = P * PACK
RUN = 8
BANK = 512
HALF = S // 2
N_TILES = N // P
QUADRANTS = 4

UNITS = [(0, 0, 512), (0, 512, 512)] + [(1, c0, 256) for c0 in range(0, S, 256)]
STEPS = [
    (u, list(range(t0, t0 + BANK // width)))
    for u, (b, c0, width) in enumerate(UNITS)
    for t0 in range(0, PACK, BANK // width)
]
EXP_LAG = 1
PRODUCT_LAG = 3
ROUND_STEPS = 10
FIRST_BANKS = 5
OUT_BANKS = 2
RING = 4


def tile_list_anaesthesia_depth_agreement_kernel(
    tc, tab_words, tab_scales, offs, xs_words, xs_scales, wa, wb_words, wb_scales,
    gain, wo, wd_words, wd_scales, bo, out,
):
    nc = tc.nc
    with ExitStack() as ctx:
        keep = ctx.enter_context(tc.tile_pool(name="keep", bufs=1))
        ring = ctx.enter_context(tc.tile_pool(name="ring", bufs=RING))
        psum = ctx.enter_context(tc.psum_pool(name="psum", bufs=1))

        def held(shape, dtype, name):
            return keep.tile(shape, dtype, name=name, align_bytes=64)

        def first_bank():
            return psum.tile([P, BANK], F32, name="first_bank", bufs=FIRST_BANKS)

        def out_bank():
            return psum.tile([P, BANK], F32, name="out_bank", bufs=OUT_BANKS)

        offsets = held([P, S // 16], U16, "offsets")
        tab_w = [held([P, T], I32, "tab_w%d" % a) for a in range(2)]
        tab_s = held([P, T], U8, "tab_s")
        wb_loaded_w = held([P, 2 * H], U8, "wb_loaded_w")
        wb_loaded_s = held([P, H], U8, "wb_loaded_s")
        wb_w = held([P, 2 * H], U8, "wb_w")
        wb_s = held([P, H], U8, "wb_s")
        xs_w = held([P, S], I32, "xs_w")
        xs_s = held([P, S], U8, "xs_s")
        wd_w = held([P, 2, N], I32, "wd_w")
        wd_s = held([P, N], U8, "wd_s")
        vector_rows = held([P, P], F32, "vector_rows")
        identity = held([P, P], F32, "identity")
        biases = held([P, N_TILES], F32, "biases")
        wa_loaded = {(a, b): held([P, PACK, PASS], F32, "wa_loaded%d%d" % (a, b)) for b in range(2) for a in range(2)}
        wo_loaded = [held([P, PACK, N], F32, "wo_loaded%d" % b) for b in range(2)]

        nc.gpsimd.memset(tab_s[:].bitcast(I32), 0)
        nc.gpsimd.memset(vector_rows[:], 0.0)
        make_identity(nc, identity[:])

        def load_scales(queue, tile, scales, quadrant):
            rows = 4 * scales.shape[0]
            queue.dma_start(
                out=tile[32 * quadrant : 32 * quadrant + rows, :].bitcast(I32),
                in_=scales[:, 4 * quadrant : 4 * quadrant + 4, :].bitcast(I32),
            )

        def load_words(tile, words):
            nc.sync.dma_start(out=tile[:], in_=words.rearrange("p c i -> p (c i)").bitcast(I32))

        def load_wa(a, b):
            rows = wa[a * PASS : (a + 1) * PASS, b * PASS : (b + 1) * PASS]
            nc.sync.dma_start(out=wa_loaded[a, b][:], in_=rows.rearrange("(p i) c -> p i c", i=PACK))

        for quadrant in range(QUADRANTS):
            load_scales(nc.sync if quadrant % 2 else nc.scalar, wb_loaded_s, wb_scales, quadrant)
        load_scales(nc.scalar, xs_s, xs_scales, 0)
        nc.sync.dma_start(out=wb_loaded_w[:].bitcast(I32), in_=wb_words[0].bitcast(I32))
        load_scales(nc.scalar, xs_s, xs_scales, 1)
        load_words(tab_w[0], tab_words[0])
        load_scales(nc.scalar, xs_s, xs_scales, 2)
        nc.sync.dma_start(offsets[:], offs)
        load_scales(nc.scalar, xs_s, xs_scales, 3)
        load_words(xs_w, xs_words[0])
        for quadrant in range(QUADRANTS):
            load_scales(nc.sync, tab_s, tab_scales, quadrant)
        load_wa(0, 0)
        load_words(tab_w[1], tab_words[1])
        load_wa(1, 0)
        gain_rows = gain.rearrange("(b q t u) -> b t q u", b=2, t=PACK, u=RUN)
        for b in range(2):
            rows = vector_rows[PACK * b : PACK * (b + 1), :]
            nc.sync.dma_start(out=rows.rearrange("t (q u) -> t q u", u=RUN), in_=gain_rows[b])
        nc.sync.dma_start(out=vector_rows[2 * PACK : 2 * PACK + N_TILES, :], in_=bo.rearrange("(n p) -> n p", p=P))
        for a in range(2):
            load_wa(a, 1)
        for b in range(2):
            slot_rows = wo[b * PASS : (b + 1) * PASS, :].rearrange("(q t u) c -> t q u c", t=PACK, u=RUN)
            for t in range(PACK):
                nc.sync.dma_start(out=wo_loaded[b][:, t, :], in_=slot_rows[t])
        nc.sync.dma_start(out=wd_w[:], in_=wd_words.rearrange("a p c i -> p a (c i)").bitcast(I32))
        for quadrant in range(QUADRANTS):
            load_scales(nc.sync, wd_s, wd_scales, quadrant)

        for quadrant in range(QUADRANTS):
            rows = slice(32 * quadrant, 32 * quadrant + 4)
            nc.vector.tensor_copy(
                out=wb_s[rows, :].bitcast(I32).rearrange("p (b t q w) -> p b t q w", b=2, t=PACK, w=RUN // 4),
                in_=wb_loaded_s[rows, :].bitcast(I32).rearrange("p (b q t w) -> p b t q w", b=2, t=PACK, w=RUN // 4),
            )
        nc.vector.tensor_copy(
            out=wb_w[:].bitcast(I32).rearrange("p (b t q w) -> p b t q w", b=2, t=PACK, w=RUN // 2),
            in_=wb_loaded_w[:].bitcast(I32).rearrange("p (b q t w) -> p b t q w", b=2, t=PACK, w=RUN // 2),
        )

        def interleave(engine, dst, src):
            if engine is nc.gpsimd:
                nc.gpsimd.tensor_scalar(dst, src, 1.0, 0.0, ALU.mult, ALU.add)
            elif engine is nc.scalar:
                nc.scalar.copy(out=dst, in_=src)
            else:
                nc.vector.tensor_copy(out=dst, in_=src)

        def quantise(name, values, columns):
            codes = held([P, columns], U32, name + "_codes")
            scales = held([P, columns], U8, name + "_scales")
            nc.vector.quantize_mx(out=codes[:].bitcast(FP8X4), scales=scales[:], in_=values)
            return codes, scales

        wa_bf = {
            (a, b, pair): held([P, 2, P, PACK], BF16, "wa_bf%d%d%d" % (a, b, pair))
            for a in range(2) for b in range(2) for pair in range(2)
        }
        wa_mx = {}

        def round_wa(a, b, t, engine):
            src = wa_loaded[a, b][:].rearrange("p i (q t u) -> p t q u i", t=PACK, u=RUN)[:, t]
            interleave(engine, wa_bf[a, b, t // 2][:, t % 2].rearrange("p (q u) i -> p q u i", u=RUN), src)

        def quantise_wa(a, b, pair):
            values = wa_bf[a, b, pair][:].rearrange("p t m i -> p (t m i)")
            wa_mx[a, b, pair] = quantise("wa%d%d%d" % (a, b, pair), values, 2 * P)

        for t in (2, 3):
            round_wa(1, 0, t, nc.scalar)

        b_kept = []
        for s, (u, slots) in enumerate(STEPS):
            b, c0, width = UNITS[u]
            bank = first_bank()
            for g, t in enumerate(slots):
                col = b * PASS + t * P
                nc.tensor.matmul_mx(
                    out=bank[:, g * width : (g + 1) * width],
                    lhsT=wb_w[:, 2 * col : 2 * (col + P)].bitcast(FP4X4),
                    lhsT_scale=wb_s[:, col : col + P],
                    rhs=xs_w[:, c0 : c0 + width].bitcast(FP8X4),
                    rhs_scale=xs_s[:, c0 : c0 + width],
                    start=True,
                    stop=True,
                )
            kept = held([P, BANK], F32, "b_kept%d" % s)
            nc.scalar.activation(out=kept[:], in_=bank[:], func=ACT.Copy)
            b_kept.append(kept)

        v_w = {(a, half): held([P, HALF], U32, "v_w%d%d" % (a, half)) for a in range(2) for half in range(2)}
        v_s = [held([P, HALF], U8, "v_s%d" % half) for half in range(2)]

        def list_half(half):
            return offsets[:, half * HALF // 16 : (half + 1) * HALF // 16]

        def gather_words(a, half):
            nc.vector.tensor_copy(v_w[a, half][:], tab_w[a][:].bitcast(U32).indirect(list_half(half)))

        def gather_scales(half):
            nc.vector.tensor_copy(v_s[half][:], tab_s[:].indirect(list_half(half)))

        def looked_up(a, c0, width):
            half, lo = divmod(c0, HALF)
            return v_w[a, half][:, lo : lo + width], v_s[half][4 * a :, lo : lo + width]

        for half in range(2):
            gather_words(0, half)
        gather_scales(0)
        for t in range(PACK):
            round_wa(0, 0, t, nc.vector)
        gather_scales(1)
        for pair in range(2):
            quantise_wa(0, 0, pair)
        gather_words(1, 0)
        for t in (0, 1):
            round_wa(1, 0, t, nc.vector)
        quantise_wa(1, 0, 0)
        gather_words(1, 1)
        quantise_wa(1, 0, 1)

        vectors = psum.tile([P, P], F32, name="vectors")
        nc.tensor.transpose(vectors[:], vector_rows[:], identity[:])
        nc.vector.tensor_copy(out=biases[:], in_=vectors[:, 2 * PACK : 2 * PACK + N_TILES])

        wo_bf = [held([P, N, PACK], BF16, "wo_bf%d" % b) for b in range(2)]
        wo_mx = {}

        def round_late_wa(a, t):
            round_wa(a, 1, t, nc.gpsimd)
            if t % 2 == 1:
                quantise_wa(a, 1, t // 2)

        def round_wo(b, n):
            cols = slice(n * P, (n + 1) * P)
            engine = nc.gpsimd if b == 1 else nc.scalar
            interleave(engine, wo_bf[b][:, cols, :], wo_loaded[b][:, :, cols].rearrange("p t c -> p c t"))
            if n == N_TILES - 1:
                wo_mx[b] = quantise("wo%d" % b, wo_bf[b][:].rearrange("p c t -> p (c t)"), N)

        late_pieces = [(round_late_wa, a, t) for a in range(2) for t in range(PACK)]
        late_pieces.extend([(round_wo, b, n) for b in range(2) for n in range(N_TILES)])

        a_banks, distances, nears, h_slots, h_mx = {}, {}, {}, {}, {}

        def difference(s):
            u, slots = STEPS[s]
            b, c0, width = UNITS[u]
            bank = first_bank()
            for g, t in enumerate(slots):
                cols = slice((t % 2) * P, (t % 2 + 1) * P)
                for a in range(2):
                    codes, scales = wa_mx[a, b, t // 2]
                    words, word_scales = looked_up(a, c0, width)
                    nc.tensor.matmul_mx(
                        out=bank[:, g * width : (g + 1) * width],
                        lhsT=codes[:, cols].bitcast(FP8X4),
                        lhsT_scale=scales[:, cols],
                        rhs=words.bitcast(FP8X4),
                        rhs_scale=word_scales,
                        start=(a == 0),
                        stop=(a == 1),
                    )
            diff = ring.tile([P, BANK], F32, name="diff")
            nc.vector.tensor_tensor(diff[:], b_kept[s][:], bank[:], ALU.subtract)
            distance = ring.tile([P, BANK], F32, name="distance")
            nc.scalar.activation(out=distance[:], in_=diff[:], func=ACT.Abs)
            a_banks[s] = bank
            distances[s] = distance

        def nearness(s):
            near = ring.tile([P, BANK], F32, name="near")
            nc.scalar.activation(out=near[:], in_=distances[s][:], func=ACT.Exp, scale=-1.0)
            nears[s] = near

        def product(s):
            u, slots = STEPS[s]
            b, c0, width = UNITS[u]
            if slots[0] == 0:
                h_slots[u] = held([P, PACK, width], BF16, "h_slots%d" % u)
            for g, t in enumerate(slots):
                cols = slice(g * width, (g + 1) * width)
                nc.vector.scalar_tensor_tensor(
                    out=h_slots[u][:, t, :],
                    in0=nears[s][:, cols],
                    scalar=vectors[:, PACK * b + t : PACK * b + t + 1],
                    in1=a_banks[s][:, cols],
                    op0=ALU.mult,
                    op1=ALU.mult,
                )

        def quantise_h(u):
            width = UNITS[u][2]
            h_bf = held([P, width, PACK], BF16, "h_bf%d" % u)
            engine, piece = (nc.vector, width) if u == len(UNITS) - 1 else (nc.gpsimd, P)
            for lo in range(0, width, piece):
                src = h_slots[u][:, :, lo : lo + piece].rearrange("p t c -> p c t")
                interleave(engine, h_bf[:, lo : lo + piece, :], src)
            h_mx[u] = quantise("h%d" % u, h_bf[:].rearrange("p c t -> p (c t)"), width)

        def second_stage(u):
            b, c0, width = UNITS[u]
            half, lo = divmod(c0, HALF)
            late = u >= len(UNITS) - 2
            h_parts = [(h_mx[half], slice(lo, lo + width)), (h_mx[u], slice(0, width))]
            per_bank = BANK // width
            for n0 in range(0, N_TILES, per_bank):
                bank = first_bank() if late else out_bank()
                rows = [slice((n0 + g) * P, (n0 + g + 1) * P) for g in range(per_bank)]
                passes = []
                for a in range(2):
                    words, word_scales = looked_up(a, c0, width)
                    for g in range(per_bank):
                        passes.append((g, wd_w[:, a, rows[g]], wd_s[4 * a :, rows[g]], words, word_scales))
                for r_pass, ((codes, scales), cols) in enumerate(h_parts):
                    wo_codes, wo_scales = wo_mx[r_pass]
                    for g in range(per_bank):
                        passes.append((g, wo_codes[:, rows[g]], wo_scales[:, rows[g]], codes[:, cols], scales[:, cols]))
                for i, (g, weights, weight_scales, moving, moving_scales) in enumerate(passes):
                    nc.tensor.matmul_mx(
                        out=bank[:, g * width : (g + 1) * width],
                        lhsT=weights.bitcast(FP8X4),
                        lhsT_scale=weight_scales,
                        rhs=moving.bitcast(FP8X4),
                        rhs_scale=moving_scales,
                        start=(i == 0),
                        stop=(i == len(passes) - 1),
                    )
                result = ring.tile([P, per_bank, width], F32, name="result")
                for g in range(per_bank):
                    bias = biases[:, n0 + g : n0 + g + 1]
                    sums = bank[:, g * width : (g + 1) * width]
                    if late and n0 > 0:
                        nc.vector.tensor_scalar(result[:, g, :], sums, bias, None, ALU.add)
                    else:
                        nc.scalar.activation(out=result[:, g, :], in_=sums, func=ACT.Identity, bias=bias)
                stored = out[n0 * P : (n0 + per_bank) * P, c0 : c0 + width]
                nc.sync.dma_start(out=stored.rearrange("(g p) c -> p g c", p=P), in_=result[:])

        for s in range(len(STEPS) + PRODUCT_LAG):
            if s < len(STEPS):
                difference(s)
            if 0 <= s - EXP_LAG < len(STEPS):
                nearness(s - EXP_LAG)
            if s >= PRODUCT_LAG:
                product(s - PRODUCT_LAG)
                u, slots = STEPS[s - PRODUCT_LAG]
                if slots[-1] == PACK - 1:
                    quantise_h(u)
                    if UNITS[u][0] == 1:
                        second_stage(u)
            if 1 <= s <= ROUND_STEPS:
                lo, hi = ((s - 1) * len(late_pieces) // ROUND_STEPS, s * len(late_pieces) // ROUND_STEPS)
                for work, first, second in late_pieces[lo:hi]:
                    work(first, second)
